import numpy as np
import ml_dtypes


def mxq(x, axis, fmt="e4m3"):
    dtype, down = {"e4m3": (ml_dtypes.float8_e4m3fn, 7), "e5m2": (ml_dtypes.float8_e5m2, 14)}[fmt]
    v = np.moveaxis(np.asarray(x, np.float32).astype(ml_dtypes.bfloat16).astype(np.float64), axis, -1)
    blocks = v.reshape(v.shape[:-1] + (-1, 32))
    amax = np.abs(blocks).max(-1, keepdims=True)
    byte = np.maximum(np.where(amax > 0, np.frexp(amax)[1] - 1 + 127, 0) - down, 1)
    scale = np.exp2(byte - 127.0)
    codes = (blocks / scale).astype(np.float32).astype(dtype).astype(np.float64)
    return np.moveaxis((codes * scale).reshape(v.shape), -1, axis)


WIDE = False


def mx_kscale(k):
    if not WIDE:
        return np.ones(k)
    levels = np.array([10, -10, 5, -5, 0])
    if k % 512:
        return np.exp2(np.random.permutation(np.resize(levels, k // 32))).repeat(32)
    a = np.empty((k // 512, 16))
    for p in range(k // 512):
        a[p, :8] = np.random.permutation(np.resize(levels, 8))
        for g in range(8):
            far = levels[np.abs(levels - a[p, g]) >= 10]
            a[p, g + 8] = far[np.random.randint(len(far))]
    return np.exp2(a.ravel()).repeat(32)


def f64(x):
    return np.asarray(x).astype(np.float64)


def striped(idx):
    return np.tile(idx.reshape(-1, 16).T, (8, 1)).astype(np.uint16)


def unstriped(offs):
    return offs[:16].T.reshape(-1).astype(np.int64)


def pack_weight(w):
    k, n = w.shape
    w = f64(np.asarray(w, np.float32).astype(ml_dtypes.bfloat16)).reshape(k // 32, 32, n)
    amax = np.abs(w).max(1)
    byte = np.clip(np.where(amax > 0, np.frexp(amax)[1] - 1 + 127 - 7, 1), 1, 254)
    scaled = (w * np.exp2(127.0 - byte)[:, None, :]).reshape(k, n).astype(np.float32)
    words = np.ascontiguousarray(scaled.reshape(k // 512, 128, 4, n).transpose(0, 1, 3, 2)).astype(ml_dtypes.float8_e4m3fn).view(np.uint8)
    return words, np.ascontiguousarray(byte.astype(np.uint8).reshape(k // 512, 16, n))


def unpack_weight(words, scales):
    g, p, n, _ = words.shape
    vals = np.ascontiguousarray(words).view(ml_dtypes.float8_e4m3fn).astype(np.float64) * np.repeat(np.exp2(scales.astype(np.float64) - 127.0), 8, axis=1)[..., None]
    return vals.transpose(0, 1, 3, 2).reshape(g * 512, n)


K, T, E, C, N = 2048, 1024, 16, 128, 128


def by_expert(wq, xq):
    return np.concatenate([wq[e].T @ xq[:, e * C:(e + 1) * C] for e in range(E)], axis=1)


def setup_inputs():
    n = np.random.standard_normal
    s = mx_kscale(K)[:, None]
    first = np.random.permutation(np.repeat(np.arange(E), T // E))
    second = (first + 1 + np.random.permutation(np.repeat(np.arange(E - 1), -(-T // (E - 1)))[:T])) % E
    while np.bincount(second, minlength=E).max() != T // E:
        load = np.bincount(second, minlength=E); hi, lo = int(load.argmax()), int(load.argmin())
        t = np.flatnonzero((second == hi) & (first != lo))[0]; second[t] = lo
    slot_token = np.empty(E * C, np.int64); pos = np.empty((2, T), np.int64); fill = np.zeros(E, np.int64)
    place = np.stack([np.random.permutation(C) for _ in range(E)])
    for r, deal in enumerate((first, second)):
        for t in np.random.permutation(T):
            e = deal[t]; j = e * C + place[e, fill[e]]; fill[e] += 1; slot_token[j] = t; pos[r, t] = j
    g = np.random.uniform(0.2, 0.8, T)
    packed = [pack_weight(m) for m in n((E, K, N)) / np.sqrt(K) / s[None]]
    return {
        "xT": (n((K, T)) * s).astype(np.float32),
        "w_words": np.stack([m[0] for m in packed]),
        "w_scales": np.stack([m[1] for m in packed]),
        "gate": np.stack([np.tile(g, (N, 1)), np.tile(1.0 - g, (N, 1))]).astype(np.float32),
        "offs": striped(slot_token),
        "pos1": striped(pos[0]),
        "pos2": striped(pos[1]),
    }


def reference(xT, w_words, w_scales, gate, offs, pos1, pos2):
    idx = unstriped(offs)
    xq = mxq(f64(xT)[:, idx], 0, "e4m3")
    w = np.stack([unpack_weight(w_words[e], w_scales[e]) for e in range(E)])
    y = by_expert(w, xq)
    return f64(gate[0]) * y[:, unstriped(pos1)] + f64(gate[1]) * y[:, unstriped(pos2)]

@@ -1,0 +1,170 @@
+from contextlib import ExitStack
+
+import concourse.mybir as mybir
+
+K, T, E, C, N = 2048, 1024, 16, 128, 128
+FLOPS = 2 * K * N * E * C
+
+F32 = mybir.dt.float32
+BF16 = mybir.dt.bfloat16
+I32 = mybir.dt.int32
+U32 = mybir.dt.uint32
+U16 = mybir.dt.uint16
+U8 = mybir.dt.uint8
+FP8X4 = mybir.dt.float8_e4m3fn_x4
+MULT = mybir.AluOpType.mult
+ADD = mybir.AluOpType.add
+
+P = 128
+PASSES = K // 512
+LAST = PASSES - 1
+SLOTS = E * C
+
+X_CUTS = ((0, 512, 768, 1024), (0, 256, 512, 768, 1024), (0, 512, 1024), (0, 512, 768, 1024))
+EARLY_CUTS = (0, 1536, 2048)
+BYTE_CUTS = (0, 768, 1536, 2048)
+LAST_CUTS = {768: (0, 768), 1536: (768, 1536), 2048: (1536, 1792, 2048)}
+OUT_CUTS = (0, 768, 1024)
+HEAD_VECTOR_COLS = {0: 320, 512: 96, 768: 160}
+EARLY_W = {(2, 512): 0, (3, 0): 1, (3, 512): 2}
+
+
+def pairs(cuts):
+    return list(zip(cuts[:-1], cuts[1:]))
+
+
+def tile_routed_moe_kernel(tc, xT, w_words, w_scales, gate, offs, pos1, pos2, out):
+    nc = tc.nc
+    with ExitStack() as ctx:
+        lists = ctx.enter_context(tc.tile_pool(name="lists", bufs=1))
+        keep = ctx.enter_context(tc.tile_pool(name="keep", bufs=1))
+        grp = ctx.enter_context(tc.tile_pool(name="grp", bufs=4))
+        psum = ctx.enter_context(tc.psum_pool(name="psum", bufs=8))
+
+        offs_t = lists.tile([P, SLOTS // 16], U16, name="offs_t")
+        pos1_t = lists.tile([P, T // 16], U16, name="pos1_t")
+        pos2_t = lists.tile([P, T // 16], U16, name="pos2_t")
+
+        codes = keep.tile([P, (PASSES + 1) * T], I32, name="codes", align_bytes=64)
+        nc.vector.memset(codes[:, PASSES * T:], 0)
+        xs = keep.tile([P, T], U8, name="xs", align_bytes=64)
+        nc.gpsimd.memset(xs[:], 0)
+        gw = keep.tile([P, PASSES, SLOTS], U32, name="gw", align_bytes=64)
+        gb = keep.tile([P, SLOTS], U8, name="gb", align_bytes=64)
+        ww = keep.tile([P, E * PASSES, N], I32, name="ww", align_bytes=64)
+        ws = keep.tile([P, E, N], U8, name="ws", align_bytes=64)
+        nc.vector.memset(ws[:].bitcast(I32), 0)
+        gate_t = keep.tile([P, 2, T], F32, name="gate_t")
+        y = keep.tile([P, SLOTS], F32, name="y")
+
+        def load_w(e0, e1):
+            nc.sync.dma_start(
+                ww[:, e0 * PASSES:e1 * PASSES, :],
+                w_words[e0:e1].rearrange("e a p n r -> p (e a) (n r)").bitcast(I32),
+            )
+
+        x_view = xT.rearrange("(a p t) n -> a p t n", p=P, t=4)
+        raws = {}
+        for a in range(PASSES):
+            for t0, t1 in pairs(X_CUTS[a]):
+                if (a, t0) in EARLY_W:
+                    load_w(EARLY_W[(a, t0)], EARLY_W[(a, t0)] + 1)
+                if a == 0 and t1 == T:
+                    nc.sync.dma_start(offs_t[:], offs)
+                raw = keep.tile([P, 4, t1 - t0], F32, name="raw%d_%d" % (a, t0))
+                nc.sync.dma_start(raw[:], x_view[a, :, :, t0:t1])
+                raws[(a, t0)] = raw
+        nc.sync.dma_start(pos1_t[:], pos1)
+        nc.sync.dma_start(pos2_t[:], pos2)
+        ws_view = w_scales.bitcast(I32)
+        for q in range(4):
+            for a in range(PASSES):
+                r0 = 32 * q + 4 * a
+                nc.sync.dma_start(ws[r0:r0 + 4, :, :].bitcast(I32), ws_view[:, a, 4 * q:4 * q + 4, :].rearrange("e r n -> r e n"))
+        for e in range(3, E):
+            load_w(e, e + 1)
+        for t0, t1 in pairs(OUT_CUTS):
+            for g in range(2):
+                nc.sync.dma_start(gate_t[:, g, t0:t1], gate[g, :, t0:t1])
+
+        def interleave(eng_copy, grouped, raw, lo, hi):
+            eng_copy(
+                out=grouped[:, lo:hi, :].rearrange("p (c i) t -> p c t i", i=4),
+                in_=raw[:, :, lo:hi].rearrange("p t (c i) -> p c t i", i=4),
+            )
+
+        def cast_quant(a, t0, t1, vector_cols):
+            w = t1 - t0
+            grouped = grp.tile([P, 512, 4], BF16, name="grouped", align_bytes=64)
+            raw = raws[(a, t0)]
+            if vector_cols > 0:
+                interleave(nc.vector.tensor_copy, grouped, raw, 0, vector_cols)
+            if vector_cols < w:
+                interleave(nc.scalar.copy, grouped, raw, vector_cols, w)
+            nc.vector.quantize_mx(
+                out=codes[:, (LAST - a) * T + t0:(LAST - a) * T + t1].bitcast(FP8X4),
+                scales=xs[4 * a:P, t0:t1],
+                in_=grouped[:, 0:w, :].rearrange("p n t -> p (n t)"),
+            )
+
+        def gather_words(a, s0, s1, blocks):
+            window = codes[:, (LAST - a) * T:(LAST - a + blocks) * T].bitcast(U32)
+            nc.vector.tensor_copy(out=gw[:, a, s0:s1], in_=window.indirect(offs_t[:, s0 // 16:s1 // 16]))
+
+        def gather_bytes(s0, s1):
+            nc.vector.tensor_copy(out=gb[:, s0:s1], in_=xs[:].indirect(offs_t[:, s0 // 16:s1 // 16]))
+
+        accs = {}
+
+        def multiply(e, a):
+            if a == 0:
+                accs[e] = psum.tile([P, C], F32, name="acc")
+            cols = slice(e * C, (e + 1) * C)
+            nc.tensor.matmul_mx(
+                out=accs[e][:],
+                lhsT=ww[:, e * PASSES + a, :].bitcast(FP8X4),
+                lhsT_scale=ws[4 * a:P, e, :],
+                rhs=gw[:, a, cols].bitcast(FP8X4),
+                rhs_scale=gb[4 * a:P, cols],
+                start=(a == 0),
+                stop=(a == LAST),
+            )
+
+        for a in range(PASSES):
+            for t0, t1 in pairs(X_CUTS[a]):
+                cast_quant(a, t0, t1, HEAD_VECTOR_COLS[t0] if a == 0 else 0)
+            if a < LAST:
+                for s0, s1 in pairs(EARLY_CUTS):
+                    gather_words(a, s0, s1, 2)
+
+        for b0, b1 in pairs(BYTE_CUTS):
+            gather_bytes(b0, b1)
+            for e in range(b0 // C, b1 // C):
+                for a in range(LAST):
+                    multiply(e, a)
+            for s0, s1 in pairs(LAST_CUTS[b1]):
+                gather_words(LAST, s0, s1, 1)
+                for e in range(s0 // C, s1 // C):
+                    multiply(e, LAST)
+                    if e == E - 1:
+                        nc.vector.tensor_copy(out=y[:, e * C:(e + 1) * C], in_=accs[e][:])
+                    else:
+                        nc.scalar.copy(out=y[:, e * C:(e + 1) * C], in_=accs[e][:])
+
+        def fetch(g, pos_t, t0, t1):
+            part = keep.tile([P, t1 - t0], F32, name="part%d_%d" % (g, t0))
+            nc.vector.tensor_tensor(out=part[:], in0=y[:].indirect(pos_t[:, t0 // 16:t1 // 16]), in1=gate_t[:, g, t0:t1], op=MULT)
+            return part
+
+        def add_store(first, second, t0, t1):
+            total = keep.tile([P, t1 - t0], F32, name="total%d" % t0)
+            nc.vector.tensor_tensor(out=total[:], in0=first[:], in1=second[:], op=ADD)
+            nc.sync.dma_start(out[:, t0:t1], total[:])
+
+        (a0, a1), (b0, b1) = pairs(OUT_CUTS)
+        first_a = fetch(0, pos1_t, a0, a1)
+        second_a = fetch(1, pos2_t, a0, a1)
+        first_b = fetch(0, pos1_t, b0, b1)
+        add_store(first_a, second_a, a0, a1)
+        second_b = fetch(1, pos2_t, b0, b1)
+        add_store(first_b, second_b, b0, b1)

@@ -26,7 +26,7 @@ BYTE_CUTS = (0, 768, 1536, 2048)
 LAST_CUTS = {768: (0, 768), 1536: (768, 1536), 2048: (1536, 1792, 2048)}
 OUT_CUTS = (0, 768, 1024)
 HEAD_VECTOR_COLS = {0: 320, 512: 96, 768: 160}
-EARLY_W = {(2, 512): 0, (3, 0): 1, (3, 512): 2}
+EARLY_W = {}
 
 
 def pairs(cuts):
@@ -81,7 +81,7 @@ def tile_routed_moe_kernel(tc, xT, w_words, w_scales, gate, offs, pos1, pos2, ou
             for a in range(PASSES):
                 r0 = 32 * q + 4 * a
                 nc.sync.dma_start(ws[r0:r0 + 4, :, :].bitcast(I32), ws_view[:, a, 4 * q:4 * q + 4, :].rearrange("e r n -> r e n"))
-        for e in range(3, E):
+        for e in range(E):
             load_w(e, e + 1)
         for t0, t1 in pairs(OUT_CUTS):
             for g in range(2):

@@ -20,7 +20,7 @@ PASSES = K // 512
 LAST = PASSES - 1
 SLOTS = E * C
 
-X_CUTS = ((0, 512, 768, 1024), (0, 256, 512, 768, 1024), (0, 512, 1024), (0, 512, 768, 1024))
+X_CUTS = ((0, 512, 768, 1024), (0, 256, 512, 768, 1024), (0, 512, 768, 1024), (0, 512, 768, 1024))
 EARLY_CUTS = (0, 1536, 2048)
 BYTE_CUTS = (0, 768, 1536, 2048)
 LAST_CUTS = {768: (0, 768), 1536: (768, 1536), 2048: (1536, 1792, 2048)}

@@ -52,7 +52,7 @@ def tile_routed_moe_kernel(tc, xT, w_words, w_scales, gate, offs, pos1, pos2, ou
         gw = keep.tile([P, PASSES, SLOTS], U32, name="gw", align_bytes=64)
         gb = keep.tile([P, SLOTS], U8, name="gb", align_bytes=64)
         ww = keep.tile([P, E * PASSES, N], I32, name="ww", align_bytes=64)
-        ws = keep.tile([P, E, N], U8, name="ws", align_bytes=64)
+        ws = keep.tile([P, E, 2 * N], U8, name="ws", align_bytes=256)
         nc.vector.memset(ws[:].bitcast(I32), 0)
         gate_t = keep.tile([P, 2, T], F32, name="gate_t")
         y = keep.tile([P, SLOTS], F32, name="y")
@@ -77,10 +77,9 @@ def tile_routed_moe_kernel(tc, xT, w_words, w_scales, gate, offs, pos1, pos2, ou
         nc.sync.dma_start(pos1_t[:], pos1)
         nc.sync.dma_start(pos2_t[:], pos2)
         ws_view = w_scales.bitcast(I32)
-        for q in range(4):
-            for a in range(PASSES):
-                r0 = 32 * q + 4 * a
-                nc.sync.dma_start(ws[r0:r0 + 4, :, :].bitcast(I32), ws_view[:, a, 4 * q:4 * q + 4, :].rearrange("e r n -> r e n"))
+        for a in range(PASSES):
+            for r in range(4):
+                nc.sync.dma_start(ws[4 * a + r:P:32, :, 0:N].bitcast(I32), ws_view[:, a, r:16:4, :].rearrange("e q n -> q e n"))
         for e in range(E):
             load_w(e, e + 1)
         for t0, t1 in pairs(OUT_CUTS):
@@ -123,7 +122,7 @@ def tile_routed_moe_kernel(tc, xT, w_words, w_scales, gate, offs, pos1, pos2, ou
             nc.tensor.matmul_mx(
                 out=accs[e][:],
                 lhsT=ww[:, e * PASSES + a, :].bitcast(FP8X4),
-                lhsT_scale=ws[4 * a:P, e, :],
+                lhsT_scale=ws[4 * a:P, e, 0:N],
                 rhs=gw[:, a, cols].bitcast(FP8X4),
                 rhs_scale=gb[4 * a:P, cols],
                 start=(a == 0),

@@ -41,9 +41,9 @@ def tile_routed_moe_kernel(tc, xT, w_words, w_scales, gate, offs, pos1, pos2, ou
         grp = ctx.enter_context(tc.tile_pool(name="grp", bufs=4))
         psum = ctx.enter_context(tc.psum_pool(name="psum", bufs=8))
 
-        offs_t = lists.tile([P, SLOTS // 16], U16, name="offs_t")
-        pos1_t = lists.tile([P, T // 16], U16, name="pos1_t")
-        pos2_t = lists.tile([P, T // 16], U16, name="pos2_t")
+        offs_t = lists.tile([P, SLOTS // 16], U16, name="offs_t", align_bytes=256)
+        pos1_t = lists.tile([P, T // 16], U16, name="pos1_t", align_bytes=256)
+        pos2_t = lists.tile([P, T // 16], U16, name="pos2_t", align_bytes=256)
 
         codes = keep.tile([P, (PASSES + 1) * T], I32, name="codes", align_bytes=64)
         nc.vector.memset(codes[:, PASSES * T:], 0)
@@ -51,10 +51,10 @@ def tile_routed_moe_kernel(tc, xT, w_words, w_scales, gate, offs, pos1, pos2, ou
         nc.gpsimd.memset(xs[:], 0)
         gw = keep.tile([P, PASSES, SLOTS], U32, name="gw", align_bytes=64)
         gb = keep.tile([P, SLOTS], U8, name="gb", align_bytes=64)
-        ww = keep.tile([P, E * PASSES, N], I32, name="ww", align_bytes=64)
+        ww = keep.tile([P, E * PASSES, N], I32, name="ww", align_bytes=256)
         ws = keep.tile([P, E, 2 * N], U8, name="ws", align_bytes=256)
         nc.vector.memset(ws[:].bitcast(I32), 0)
-        gate_t = keep.tile([P, 2, T], F32, name="gate_t")
+        gate_t = keep.tile([P, 2, T], F32, name="gate_t", align_bytes=256)
         y = keep.tile([P, SLOTS], F32, name="y")
 
         def load_w(e0, e1):
@@ -71,7 +71,7 @@ def tile_routed_moe_kernel(tc, xT, w_words, w_scales, gate, offs, pos1, pos2, ou
                     load_w(EARLY_W[(a, t0)], EARLY_W[(a, t0)] + 1)
                 if a == 0 and t1 == T:
                     nc.sync.dma_start(offs_t[:], offs)
-                raw = keep.tile([P, 4, t1 - t0], F32, name="raw%d_%d" % (a, t0))
+                raw = keep.tile([P, 4, t1 - t0], F32, name="raw%d_%d" % (a, t0), align_bytes=256)
                 nc.sync.dma_start(raw[:], x_view[a, :, :, t0:t1])
                 raws[(a, t0)] = raw
         nc.sync.dma_start(pos1_t[:], pos1)
@@ -156,7 +156,7 @@ def tile_routed_moe_kernel(tc, xT, w_words, w_scales, gate, offs, pos1, pos2, ou
             return part
 
         def add_store(first, second, t0, t1):
-            total = keep.tile([P, t1 - t0], F32, name="total%d" % t0)
+            total = keep.tile([P, t1 - t0], F32, name="total%d" % t0, align_bytes=256)
             nc.vector.tensor_tensor(out=total[:], in0=first[:], in1=second[:], op=ADD)
             nc.sync.dma_start(out[:, t0:t1], total[:])
 

from contextlib import ExitStack

import concourse.mybir as mybir

K, T, E, C, N = 2048, 1024, 16, 128, 128
FLOPS = 2 * K * N * E * C

F32 = mybir.dt.float32
BF16 = mybir.dt.bfloat16
I32 = mybir.dt.int32
U32 = mybir.dt.uint32
U16 = mybir.dt.uint16
U8 = mybir.dt.uint8
FP8X4 = mybir.dt.float8_e4m3fn_x4
MULT = mybir.AluOpType.mult
ADD = mybir.AluOpType.add

P = 128
PASSES = K // 512
LAST = PASSES - 1
SLOTS = E * C

X_CUTS = ((0, 512, 768, 1024), (0, 256, 512, 768, 1024), (0, 512, 768, 1024), (0, 512, 768, 1024))
EARLY_CUTS = (0, 1536, 2048)
BYTE_CUTS = (0, 768, 1536, 2048)
LAST_CUTS = {768: (0, 768), 1536: (768, 1536), 2048: (1536, 1792, 2048)}
OUT_CUTS = (0, 768, 1024)
HEAD_VECTOR_COLS = {0: 320, 512: 96, 768: 160}
EARLY_W = {}


def pairs(cuts):
    return list(zip(cuts[:-1], cuts[1:]))


def tile_routed_moe_kernel(tc, xT, w_words, w_scales, gate, offs, pos1, pos2, out):
    nc = tc.nc
    with ExitStack() as ctx:
        lists = ctx.enter_context(tc.tile_pool(name="lists", bufs=1))
        keep = ctx.enter_context(tc.tile_pool(name="keep", bufs=1))
        grp = ctx.enter_context(tc.tile_pool(name="grp", bufs=4))
        psum = ctx.enter_context(tc.psum_pool(name="psum", bufs=8))

        offs_t = lists.tile([P, SLOTS // 16], U16, name="offs_t", align_bytes=256)
        pos1_t = lists.tile([P, T // 16], U16, name="pos1_t", align_bytes=256)
        pos2_t = lists.tile([P, T // 16], U16, name="pos2_t", align_bytes=256)

        codes = keep.tile([P, (PASSES + 1) * T], I32, name="codes", align_bytes=64)
        nc.vector.memset(codes[:, PASSES * T:], 0)
        xs = keep.tile([P, T], U8, name="xs", align_bytes=64)
        nc.gpsimd.memset(xs[:], 0)
        gw = keep.tile([P, PASSES, SLOTS], U32, name="gw", align_bytes=64)
        gb = keep.tile([P, SLOTS], U8, name="gb", align_bytes=64)
        ww = keep.tile([P, E * PASSES, N], I32, name="ww", align_bytes=256)
        ws = keep.tile([P, E, 2 * N], U8, name="ws", align_bytes=256)
        nc.vector.memset(ws[:].bitcast(I32), 0)
        gate_t = keep.tile([P, 2, T], F32, name="gate_t", align_bytes=256)
        y = keep.tile([P, SLOTS], F32, name="y")

        def load_w(e0, e1):
            nc.sync.dma_start(
                ww[:, e0 * PASSES:e1 * PASSES, :],
                w_words[e0:e1].rearrange("e a p n r -> p (e a) (n r)").bitcast(I32),
            )

        x_view = xT.rearrange("(a p t) n -> a p t n", p=P, t=4)
        raws = {}
        for a in range(PASSES):
            for t0, t1 in pairs(X_CUTS[a]):
                if (a, t0) in EARLY_W:
                    load_w(EARLY_W[(a, t0)], EARLY_W[(a, t0)] + 1)
                if a == 0 and t1 == T:
                    nc.sync.dma_start(offs_t[:], offs)
                raw = keep.tile([P, 4, t1 - t0], F32, name="raw%d_%d" % (a, t0), align_bytes=256)
                nc.sync.dma_start(raw[:], x_view[a, :, :, t0:t1])
                raws[(a, t0)] = raw
        nc.sync.dma_start(pos1_t[:], pos1)
        nc.sync.dma_start(pos2_t[:], pos2)
        ws_view = w_scales.bitcast(I32)
        for a in range(PASSES):
            for r in range(4):
                nc.sync.dma_start(ws[4 * a + r:P:32, :, 0:N].bitcast(I32), ws_view[:, a, r:16:4, :].rearrange("e q n -> q e n"))
        for e in range(E):
            load_w(e, e + 1)
        for t0, t1 in pairs(OUT_CUTS):
            for g in range(2):
                nc.sync.dma_start(gate_t[:, g, t0:t1], gate[g, :, t0:t1])

        def interleave(eng_copy, grouped, raw, lo, hi):
            eng_copy(
                out=grouped[:, lo:hi, :].rearrange("p (c i) t -> p c t i", i=4),
                in_=raw[:, :, lo:hi].rearrange("p t (c i) -> p c t i", i=4),
            )

        def cast_quant(a, t0, t1, vector_cols):
            w = t1 - t0
            grouped = grp.tile([P, 512, 4], BF16, name="grouped", align_bytes=64)
            raw = raws[(a, t0)]
            if vector_cols > 0:
                interleave(nc.vector.tensor_copy, grouped, raw, 0, vector_cols)
            if vector_cols < w:
                interleave(nc.scalar.copy, grouped, raw, vector_cols, w)
            nc.vector.quantize_mx(
                out=codes[:, (LAST - a) * T + t0:(LAST - a) * T + t1].bitcast(FP8X4),
                scales=xs[4 * a:P, t0:t1],
                in_=grouped[:, 0:w, :].rearrange("p n t -> p (n t)"),
            )

        def gather_words(a, s0, s1, blocks):
            window = codes[:, (LAST - a) * T:(LAST - a + blocks) * T].bitcast(U32)
            nc.vector.tensor_copy(out=gw[:, a, s0:s1], in_=window.indirect(offs_t[:, s0 // 16:s1 // 16]))

        def gather_bytes(s0, s1):
            nc.vector.tensor_copy(out=gb[:, s0:s1], in_=xs[:].indirect(offs_t[:, s0 // 16:s1 // 16]))

        accs = {}

        def multiply(e, a):
            if a == 0:
                accs[e] = psum.tile([P, C], F32, name="acc")
            cols = slice(e * C, (e + 1) * C)
            nc.tensor.matmul_mx(
                out=accs[e][:],
                lhsT=ww[:, e * PASSES + a, :].bitcast(FP8X4),
                lhsT_scale=ws[4 * a:P, e, 0:N],
                rhs=gw[:, a, cols].bitcast(FP8X4),
                rhs_scale=gb[4 * a:P, cols],
                start=(a == 0),
                stop=(a == LAST),
            )

        for a in range(PASSES):
            for t0, t1 in pairs(X_CUTS[a]):
                cast_quant(a, t0, t1, HEAD_VECTOR_COLS[t0] if a == 0 else 0)
            if a < LAST:
                for s0, s1 in pairs(EARLY_CUTS):
                    gather_words(a, s0, s1, 2)

        for b0, b1 in pairs(BYTE_CUTS):
            gather_bytes(b0, b1)
            for e in range(b0 // C, b1 // C):
                for a in range(LAST):
                    multiply(e, a)
            for s0, s1 in pairs(LAST_CUTS[b1]):
                gather_words(LAST, s0, s1, 1)
                for e in range(s0 // C, s1 // C):
                    multiply(e, LAST)
                    if e == E - 1:
                        nc.vector.tensor_copy(out=y[:, e * C:(e + 1) * C], in_=accs[e][:])
                    else:
                        nc.scalar.copy(out=y[:, e * C:(e + 1) * C], in_=accs[e][:])

        def fetch(g, pos_t, t0, t1):
            part = keep.tile([P, t1 - t0], F32, name="part%d_%d" % (g, t0))
            nc.vector.tensor_tensor(out=part[:], in0=y[:].indirect(pos_t[:, t0 // 16:t1 // 16]), in1=gate_t[:, g, t0:t1], op=MULT)
            return part

        def add_store(first, second, t0, t1):
            total = keep.tile([P, t1 - t0], F32, name="total%d" % t0, align_bytes=256)
            nc.vector.tensor_tensor(out=total[:], in0=first[:], in1=second[:], op=ADD)
            nc.sync.dma_start(out[:, t0:t1], total[:])

        (a0, a1), (b0, b1) = pairs(OUT_CUTS)
        first_a = fetch(0, pos1_t, a0, a1)
        second_a = fetch(1, pos2_t, a0, a1)
        first_b = fetch(0, pos1_t, b0, b1)
        add_store(first_a, second_a, a0, a1)
        second_b = fetch(1, pos2_t, b0, b1)
        add_store(first_b, second_b, b0, b1)
